import numpy as np
import ml_dtypes


def mxq(x, axis, fmt="e4m3"):
    dtype, down = {"e4m3": (ml_dtypes.float8_e4m3fn, 7), "e5m2": (ml_dtypes.float8_e5m2, 14)}[fmt]
    v = np.moveaxis(np.asarray(x, np.float32).astype(ml_dtypes.bfloat16).astype(np.float64), axis, -1)
    blocks = v.reshape(v.shape[:-1] + (-1, 32))
    amax = np.abs(blocks).max(-1, keepdims=True)
    byte = np.maximum(np.where(amax > 0, np.frexp(amax)[1] - 1 + 127, 0) - down, 1)
    scale = np.exp2(byte - 127.0)
    codes = (blocks / scale).astype(np.float32).astype(dtype).astype(np.float64)
    return np.moveaxis((codes * scale).reshape(v.shape), -1, axis)


WIDE = False


def mx_kscale(k):
    if not WIDE:
        return np.ones(k)
    levels = np.array([10, -10, 5, -5, 0])
    if k % 512:
        return np.exp2(np.random.permutation(np.resize(levels, k // 32))).repeat(32)
    a = np.empty((k // 512, 16))
    for p in range(k // 512):
        a[p, :8] = np.random.permutation(np.resize(levels, 8))
        for g in range(8):
            far = levels[np.abs(levels - a[p, g]) >= 10]
            a[p, g + 8] = far[np.random.randint(len(far))]
    return np.exp2(a.ravel()).repeat(32)


def f64(x):
    return np.asarray(x).astype(np.float64)


def striped(idx):
    return np.tile(np.asarray(idx).reshape(-1, 16).T, (8, 1)).astype(np.uint16)


def unstriped(offs):
    return offs[:16].T.reshape(-1).astype(np.int64)


E2M1 = np.array([0.0, 0.5, 1.0, 1.5, 2.0, 3.0, 4.0, 6.0, -0.0, -0.5, -1.0, -1.5, -2.0, -3.0, -4.0, -6.0])


def pack_weight(w, fmt):
    k, n = w.shape
    w = f64(np.asarray(w, np.float32).astype(ml_dtypes.bfloat16)).reshape(k // 32, 32, n)
    amax = np.abs(w).max(1)
    if fmt == "e4m3":
        byte = np.frexp(amax)[1] - 1 + 127 - 7
    else:
        mant, ex = np.frexp(amax / 6.0)
        byte = np.where(mant > 0.5, ex, ex - 1) + 127
    byte = np.clip(np.where(amax > 0, byte, 1), 1, 254)
    scaled = (w * np.exp2(127.0 - byte)[:, None, :]).reshape(k, n).astype(np.float32)
    by_word = np.ascontiguousarray(scaled.reshape(k // 512, 128, 4, n).transpose(0, 1, 3, 2))
    if fmt == "e4m3":
        words = by_word.astype(ml_dtypes.float8_e4m3fn).view(np.uint8)
    else:
        c = by_word.astype(ml_dtypes.float4_e2m1fn).view(np.uint8) & 0xF
        words = (c[..., 0::2] | (c[..., 1::2] << 4)).reshape(k // 512, 128, 2 * n)
    return np.ascontiguousarray(words), np.ascontiguousarray(byte.astype(np.uint8).reshape(k // 512, 16, n))


def unpack_weight(words, scales, fmt):
    g, _, n = scales.shape
    words = np.ascontiguousarray(words).reshape(g, 128, n, -1)
    if fmt == "e4m3":
        vals = words.view(ml_dtypes.float8_e4m3fn).astype(np.float64)
    else:
        nib = np.empty((g, 128, n, 4), np.uint8)
        nib[..., 0::2] = words & 0xF
        nib[..., 1::2] = words >> 4
        vals = E2M1[nib]
    vals = vals * np.repeat(np.exp2(scales.astype(np.float64) - 127.0), 8, axis=1)[..., None]
    return vals.transpose(0, 1, 3, 2).reshape(g * 512, n)


D, T, I, Q, E = 512, 2048, 512, 128, 512


def setup_inputs():
    n = np.random.standard_normal
    idx = np.random.permutation(T)[:I]
    fd = mx_kscale(D)
    fi = mx_kscale(I)
    ti = np.ones(T)
    ti[idx] = fi
    keysp = pack_weight(n((D, T)) / fd[:, None], "e4m3")
    return {
        "query": (n((D, Q)) * 0.5 / np.sqrt(D) * fd[:, None]).astype(np.float32),
        "keys_words": keysp[0],
        "keys_scales": keysp[1],
        "prior": np.tile(np.random.uniform(0.5, 1.5, T) / 512, (128, 1)).astype(np.float32),
        "size": (np.random.uniform(4.0, 16.0, (1, I)) * fi).astype(np.float32),
        "vals": (n((E, T)) / ti).astype(np.float32),
        "offs": striped(idx),
    }


def reference(query, keys_words, keys_scales, prior, size, vals, offs):
    idx = unstriped(offs)
    keysu = unpack_weight(keys_words, keys_scales, "e4m3")
    queryq = mxq(f64(query), 0, "e4m3")
    keysidxg = keysu[:, idx]
    a = queryq.T @ keysidxg
    p = np.exp(a - np.max(a, axis=1, keepdims=True))
    w = (p / np.sum(p, axis=1, keepdims=True) - f64(prior)[:1][:, idx]) * f64(size)
    wt = w.T
    vt = f64(vals)[:, idx].T
    wtq = mxq(wt, 0, "e4m3")
    vtq = mxq(vt, 0, "e4m3")
    o = wtq.T @ vtq
    return o

@@ -1,0 +1,195 @@
+from contextlib import ExitStack
+
+import concourse.mybir as mybir
+from concourse.masks import make_identity
+
+D, T, I, Q, E = 512, 2048, 512, 128, 512
+FLOPS = 2 * D * Q * I + 2 * I * Q * E
+BYTES = 4 * (D * Q + T + I + E * T + Q * E) + D * T + 16 * T + 2 * 128 * 32
+
+F32 = mybir.dt.float32
+BF16 = mybir.dt.bfloat16
+I32 = mybir.dt.int32
+U32 = mybir.dt.uint32
+U16 = mybir.dt.uint16
+U8 = mybir.dt.uint8
+FP8X4 = mybir.dt.float8_e4m3fn_x4
+ALU = mybir.AluOpType
+ACT = mybir.ActivationFunctionType
+AXIS = mybir.AxisListType
+
+P = 128
+PACK = 4
+BLOCKS = E // P
+PRIOR_ROW = P - 1
+VECTOR_SLOTS = 256
+
+
+def tile_attend_overaverage_kernel(tc, query, keys_words, keys_scales, prior, size, vals, offs, out):
+    nc = tc.nc
+    with ExitStack() as ctx:
+        sb = ctx.enter_context(tc.tile_pool(name="sb", bufs=1))
+        ps = ctx.enter_context(tc.psum_pool(name="ps", bufs=1))
+
+        offsets = sb.tile([P, I // 16], U16, name="offsets")
+        nc.sync.dma_start(offsets[:], offs)
+
+        key_words = sb.tile([P, T], U32, name="key_words", align_bytes=64)
+        words_hbm = keys_words[0].rearrange("p t r -> p (t r)").bitcast(I32)
+        nc.sync.dma_start(key_words[:, 0 : T // 2].bitcast(I32), words_hbm[:, 0 : T // 2])
+
+        key_scales = sb.tile([P, T], U8, name="key_scales", align_bytes=64)
+        nc.vector.memset(key_scales[:].bitcast(I32), 0)
+        for quad in range(4):
+            nc.sync.dma_start(
+                key_scales[32 * quad : 32 * quad + 4, :].bitcast(I32),
+                keys_scales[0, 4 * quad : 4 * quad + 4, :].bitcast(I32),
+            )
+
+        prior_pool = sb.tile([P, T], F32, name="prior_pool", tag="after_prior")
+        nc.vector.memset(prior_pool[:], 0.0)
+        nc.scalar.dma_start(prior_pool[PRIOR_ROW:P, :], prior[0:1, :])
+
+        query_raw = sb.tile([P, PACK, Q], F32, name="query_raw")
+        nc.gpsimd.dma_start(query_raw[:], query.rearrange("(p j) q -> p j q", j=PACK))
+        nc.sync.dma_start(key_words[:, T // 2 : T].bitcast(I32), words_hbm[:, T // 2 : T])
+
+        size_col = sb.tile([P, PACK], F32, name="size_col")
+        nc.gpsimd.dma_start(size_col[:], size.rearrange("o (s r) -> (o s) r", r=PACK))
+
+        val_pools = []
+        for b in range(BLOCKS):
+            pool_tile = sb.tile([P, T], F32, name="val_pool%d" % b)
+            nc.sync.dma_start(pool_tile[:], vals[b * P : (b + 1) * P, :])
+            val_pools.append(pool_tile)
+
+        identity = sb.tile([P, P], F32, name="identity")
+        make_identity(nc, identity[:])
+
+        listed_scales = sb.tile([P, I], U8, name="listed_scales", align_bytes=64)
+        nc.vector.tensor_copy(listed_scales[:], key_scales[:].indirect(offsets[:]))
+
+        query_bf = sb.tile([P, Q, PACK], BF16, name="query_bf", align_bytes=64)
+        nc.vector.tensor_copy(query_bf[:], query_raw[:].rearrange("p j q -> p q j"))
+        query_codes = sb.tile([P, Q], U32, name="query_codes", align_bytes=64)
+        query_scales = sb.tile([P, Q], U8, name="query_scales", align_bytes=64)
+        nc.vector.quantize_mx(
+            out=query_codes[:].bitcast(FP8X4),
+            scales=query_scales[:],
+            in_=query_bf[:].rearrange("p q j -> p (q j)"),
+        )
+
+        listed_words = sb.tile([P, I], U32, name="listed_words", align_bytes=64)
+        nc.vector.tensor_copy(listed_words[:], key_words[:].indirect(offsets[:]))
+
+        scores = ps.tile([P, I], F32, name="scores")
+        nc.tensor.matmul_mx(
+            out=scores[:],
+            lhsT=query_codes[:].bitcast(FP8X4),
+            lhsT_scale=query_scales[:],
+            rhs=listed_words[:].bitcast(FP8X4),
+            rhs_scale=listed_scales[:],
+            start=True,
+            stop=True,
+        )
+
+        listed_prior = sb.tile([P, I], F32, name="listed_prior")
+        nc.scalar.activation(listed_prior[:], prior_pool[:].indirect(offsets[:]), ACT.Copy)
+        prior_turned = ps.tile([P, PACK, P], F32, name="prior_turned")
+        for r in range(PACK):
+            nc.tensor.transpose(prior_turned[:, r, :], listed_prior[:, r:I:PACK], identity[:])
+        prior_col = sb.tile([P, PACK], F32, name="prior_col")
+        nc.scalar.copy(prior_col[:], prior_turned[:, :, PRIOR_ROW])
+        prior_rows = ps.tile([P, PACK, P], F32, name="prior_rows")
+        for r in range(PACK):
+            nc.tensor.transpose(
+                prior_rows[:, r, :], prior_col[:, r : r + 1].to_broadcast([P, P]), identity[:]
+            )
+
+        neg_max = sb.tile([P, 1], F32, name="neg_max", tag="after_exp", align_bytes=64)
+        nc.vector.tensor_reduce(neg_max[:], scores[:], AXIS.X, ALU.max, negate=True)
+        probs = sb.tile([P, PACK, P], F32, name="probs", tag="after_prior")
+        row_sum = sb.tile([P, 1], F32, name="row_sum")
+        nc.scalar.activation(
+            probs[:],
+            scores[:].rearrange("q (s r) -> q r s", r=PACK),
+            ACT.Exp,
+            bias=neg_max[:],
+            accum_out=row_sum[:],
+        )
+        inv_sum = sb.tile([P, 1], F32, name="inv_sum")
+        nc.vector.reciprocal(inv_sum[:], row_sum[:])
+        excess = sb.tile([P, PACK, P], F32, name="excess", tag="after_turn", align_bytes=64)
+        nc.vector.scalar_tensor_tensor(
+            excess[:].rearrange("q r s -> q (r s)"),
+            probs[:].rearrange("q r s -> q (r s)"),
+            inv_sum[:],
+            prior_rows[:].rearrange("q r s -> q (r s)"),
+            ALU.mult,
+            ALU.subtract,
+        )
+        excess_turned = ps.tile([P, PACK, Q], F32, name="excess_turned")
+        for r in range(PACK):
+            nc.tensor.transpose(excess_turned[:, r, :], excess[:, r, :], identity[:])
+        weights_bf = sb.tile([P, Q, PACK], BF16, name="weights_bf", tag="after_weights", align_bytes=64)
+        nc.vector.tensor_tensor(
+            weights_bf[:],
+            excess_turned[:].rearrange("s r q -> s q r"),
+            size_col[:].unsqueeze(1).to_broadcast([P, Q, PACK]),
+            ALU.mult,
+        )
+        weight_codes = sb.tile([P, Q], U32, name="weight_codes", align_bytes=64)
+        weight_scales = sb.tile([P, Q], U8, name="weight_scales", align_bytes=64)
+        nc.vector.quantize_mx(
+            out=weight_codes[:].bitcast(FP8X4),
+            scales=weight_scales[:],
+            in_=weights_bf[:].rearrange("s q r -> s (q r)"),
+        )
+
+        held = ["after_exp", "after_exp", "after_weights", "turned2"]
+        early = (BLOCKS - 1) * P
+        result_early = sb.tile([P, early], F32, name="result_early")
+        result_last = sb.tile([P, P], F32, name="result_last")
+        sums_early = ps.tile([P, early], F32, name="sums_early")
+        sums_last = ps.tile([P, P], F32, name="sums_last")
+        for b in range(BLOCKS):
+            last = b == BLOCKS - 1
+            listed_vals = sb.tile([P, I], BF16, name="listed_vals%d" % b, tag=held[b], align_bytes=64)
+            window = val_pools[b]
+            if b >= BLOCKS - 2:
+                cut = VECTOR_SLOTS
+                nc.vector.tensor_copy(listed_vals[:, 0:cut], window[:].indirect(offsets[:, 0 : cut // 16]))
+                nc.scalar.activation(
+                    listed_vals[:, cut:I], window[:].indirect(offsets[:, cut // 16 : I // 16]), ACT.Copy
+                )
+            else:
+                nc.scalar.activation(listed_vals[:], window[:].indirect(offsets[:]), ACT.Copy)
+            pairs = listed_vals[:].bitcast(F32)
+            vals_turned = ps.tile([P, 2, P], F32, name="vals_turned", tag="vals_turned", bufs=2)
+            for u in range(2):
+                nc.tensor.transpose(vals_turned[:, u, :], pairs[:, u : I // 2 : 2], identity[:])
+            vals_bf = sb.tile([P, P, 2], F32, name="vals_bf%d" % b, tag="turned%d" % b, align_bytes=64)
+            nc.scalar.copy(vals_bf[:], vals_turned[:].rearrange("s u e -> s e u"))
+            val_codes = sb.tile([P, P], U32, name="val_codes%d" % b, align_bytes=64)
+            val_scales = sb.tile([P, P], U8, name="val_scales%d" % b, align_bytes=64)
+            nc.vector.quantize_mx(
+                out=val_codes[:].bitcast(FP8X4),
+                scales=val_scales[:],
+                in_=vals_bf[:].rearrange("s e u -> s (e u)").bitcast(BF16),
+            )
+            sums = sums_last[:] if last else sums_early[:, b * P : (b + 1) * P]
+            nc.tensor.matmul_mx(
+                out=sums,
+                lhsT=weight_codes[:].bitcast(FP8X4),
+                lhsT_scale=weight_scales[:],
+                rhs=val_codes[:].bitcast(FP8X4),
+                rhs_scale=val_scales[:],
+                start=True,
+                stop=True,
+            )
+            if b == BLOCKS - 2:
+                nc.vector.tensor_copy(result_early[:], sums_early[:])
+                nc.sync.dma_start(out[:, 0:early], result_early[:])
+            if last:
+                nc.vector.tensor_copy(result_last[:], sums_last[:])
+                nc.sync.dma_start(out[:, early:E], result_last[:])

@@ -34,7 +34,10 @@ def tile_attend_overaverage_kernel(tc, query, keys_words, keys_scales, prior, si
         offsets = sb.tile([P, I // 16], U16, name="offsets")
         nc.sync.dma_start(offsets[:], offs)
 
-        key_words = sb.tile([P, T], U32, name="key_words", align_bytes=64)
+        prior_pool = sb.tile([P, T], F32, name="prior_pool", tag="after_prior", align_bytes=64)
+        nc.sync.dma_start(prior_pool[PRIOR_ROW:P, :], prior[0:1, :])
+
+        key_words = sb.tile([P, T], U32, name="key_words", tag="key_words", align_bytes=64)
         words_hbm = keys_words[0].rearrange("p t r -> p (t r)").bitcast(I32)
         nc.sync.dma_start(key_words[:, 0 : T // 2].bitcast(I32), words_hbm[:, 0 : T // 2])
 
@@ -46,32 +49,35 @@ def tile_attend_overaverage_kernel(tc, query, keys_words, keys_scales, prior, si
                 keys_scales[0, 4 * quad : 4 * quad + 4, :].bitcast(I32),
             )
 
-        prior_pool = sb.tile([P, T], F32, name="prior_pool", tag="after_prior")
-        nc.vector.memset(prior_pool[:], 0.0)
-        nc.scalar.dma_start(prior_pool[PRIOR_ROW:P, :], prior[0:1, :])
+        nc.vector.memset(prior_pool[0:PRIOR_ROW, :], 0.0)
 
         query_raw = sb.tile([P, PACK, Q], F32, name="query_raw")
-        nc.gpsimd.dma_start(query_raw[:], query.rearrange("(p j) q -> p j q", j=PACK))
         nc.sync.dma_start(key_words[:, T // 2 : T].bitcast(I32), words_hbm[:, T // 2 : T])
+        nc.sync.dma_start(query_raw[:], query.rearrange("(p j) q -> p j q", j=PACK))
 
         size_col = sb.tile([P, PACK], F32, name="size_col")
         nc.gpsimd.dma_start(size_col[:], size.rearrange("o (s r) -> (o s) r", r=PACK))
 
         val_pools = []
         for b in range(BLOCKS):
-            pool_tile = sb.tile([P, T], F32, name="val_pool%d" % b)
+            pool_tile = sb.tile([P, T], F32, name="val_pool%d" % b, tag="pool%d" % b, align_bytes=64)
             nc.sync.dma_start(pool_tile[:], vals[b * P : (b + 1) * P, :])
             val_pools.append(pool_tile)
 
         identity = sb.tile([P, P], F32, name="identity")
         make_identity(nc, identity[:])
 
+        listed_prior = sb.tile([P, I], F32, name="listed_prior")
+        nc.scalar.activation(listed_prior[:], prior_pool[:].indirect(offsets[:]), ACT.Copy)
         listed_scales = sb.tile([P, I], U8, name="listed_scales", align_bytes=64)
         nc.vector.tensor_copy(listed_scales[:], key_scales[:].indirect(offsets[:]))
 
-        query_bf = sb.tile([P, Q, PACK], BF16, name="query_bf", align_bytes=64)
-        nc.vector.tensor_copy(query_bf[:], query_raw[:].rearrange("p j q -> p q j"))
-        query_codes = sb.tile([P, Q], U32, name="query_codes", align_bytes=64)
+        listed_words = sb.tile([P, I], U32, name="listed_words", tag="after_scores", align_bytes=64)
+        nc.vector.tensor_copy(listed_words[:], key_words[:].indirect(offsets[:]))
+
+        query_bf = sb.tile([P, Q, PACK], BF16, name="query_bf", tag="after_prior", align_bytes=64)
+        nc.scalar.copy(query_bf[:], query_raw[:].rearrange("p j q -> p q j"))
+        query_codes = sb.tile([P, Q], U32, name="query_codes", tag="key_words", align_bytes=64)
         query_scales = sb.tile([P, Q], U8, name="query_scales", align_bytes=64)
         nc.vector.quantize_mx(
             out=query_codes[:].bitcast(FP8X4),
@@ -79,10 +85,7 @@ def tile_attend_overaverage_kernel(tc, query, keys_words, keys_scales, prior, si
             in_=query_bf[:].rearrange("p q j -> p (q j)"),
         )
 
-        listed_words = sb.tile([P, I], U32, name="listed_words", align_bytes=64)
-        nc.vector.tensor_copy(listed_words[:], key_words[:].indirect(offsets[:]))
-
-        scores = ps.tile([P, I], F32, name="scores")
+        scores = ps.tile([P, I], F32, name="scores", tag="scores")
         nc.tensor.matmul_mx(
             out=scores[:],
             lhsT=query_codes[:].bitcast(FP8X4),
@@ -93,23 +96,59 @@ def tile_attend_overaverage_kernel(tc, query, keys_words, keys_scales, prior, si
             stop=True,
         )
 
-        listed_prior = sb.tile([P, I], F32, name="listed_prior")
-        nc.scalar.activation(listed_prior[:], prior_pool[:].indirect(offsets[:]), ACT.Copy)
-        prior_turned = ps.tile([P, PACK, P], F32, name="prior_turned")
+        prior_turned = ps.tile([P, PACK, P], F32, name="prior_turned", tag="prior_turned")
         for r in range(PACK):
             nc.tensor.transpose(prior_turned[:, r, :], listed_prior[:, r:I:PACK], identity[:])
-        prior_col = sb.tile([P, PACK], F32, name="prior_col")
-        nc.scalar.copy(prior_col[:], prior_turned[:, :, PRIOR_ROW])
-        prior_rows = ps.tile([P, PACK, P], F32, name="prior_rows")
+        prior_col = sb.tile([P, PACK], F32, name="prior_col", tag="after_scores", align_bytes=64)
+        nc.vector.tensor_copy(prior_col[:], prior_turned[:, :, PRIOR_ROW])
+        prior_rows = ps.tile([P, PACK, P], F32, name="prior_rows", tag="prior_rows")
         for r in range(PACK):
             nc.tensor.transpose(
                 prior_rows[:, r, :], prior_col[:, r : r + 1].to_broadcast([P, P]), identity[:]
             )
 
+        held = ["listed0", "pool0", "listed2", "turned2"]
+        code_tags = ["after_turn", "after_weights", "codes2", "codes3"]
+        banks = ["prior_turned", "turned1", "prior_rows", "scores"]
+
+        def gather_values(b):
+            listed_vals = sb.tile([P, I], BF16, name="listed_vals%d" % b, tag=held[b], align_bytes=64)
+            window = val_pools[b]
+            if b >= 1:
+                cut = VECTOR_SLOTS
+                nc.vector.tensor_copy(listed_vals[:, 0:cut], window[:].indirect(offsets[:, 0 : cut // 16]))
+                nc.scalar.activation(
+                    listed_vals[:, cut:I], window[:].indirect(offsets[:, cut // 16 : I // 16]), ACT.Copy
+                )
+            else:
+                nc.scalar.activation(listed_vals[:], window[:].indirect(offsets[:]), ACT.Copy)
+            return listed_vals
+
+        def turn_values(b, listed_vals):
+            pairs = listed_vals[:].bitcast(F32)
+            vals_turned = ps.tile([P, 2, P], F32, name="vals_turned%d" % b, tag=banks[b])
+            for u in range(2):
+                nc.tensor.transpose(vals_turned[:, u, :], pairs[:, u : I // 2 : 2], identity[:])
+            vals_bf = sb.tile([P, P, 2], F32, name="vals_bf%d" % b, tag="turned%d" % b, align_bytes=64)
+            nc.scalar.copy(vals_bf[:], vals_turned[:].rearrange("s u e -> s e u"))
+            return vals_bf
+
+        def quantise_values(b, vals_bf):
+            val_codes = sb.tile([P, P], U32, name="val_codes%d" % b, tag=code_tags[b], align_bytes=64)
+            val_scales = sb.tile([P, P], U8, name="val_scales%d" % b, align_bytes=64)
+            nc.vector.quantize_mx(
+                out=val_codes[:].bitcast(FP8X4),
+                scales=val_scales[:],
+                in_=vals_bf[:].rearrange("s e u -> s (e u)").bitcast(BF16),
+            )
+            return val_codes, val_scales
+
+        listed0 = gather_values(0)
+
         neg_max = sb.tile([P, 1], F32, name="neg_max", tag="after_exp", align_bytes=64)
         nc.vector.tensor_reduce(neg_max[:], scores[:], AXIS.X, ALU.max, negate=True)
-        probs = sb.tile([P, PACK, P], F32, name="probs", tag="after_prior")
-        row_sum = sb.tile([P, 1], F32, name="row_sum")
+        probs = sb.tile([P, PACK, P], F32, name="probs", tag="pool0", align_bytes=64)
+        row_sum = sb.tile([P, 1], F32, name="row_sum", tag="ring", align_bytes=64)
         nc.scalar.activation(
             probs[:],
             scores[:].rearrange("q (s r) -> q r s", r=PACK),
@@ -128,7 +167,7 @@ def tile_attend_overaverage_kernel(tc, query, keys_words, keys_scales, prior, si
             ALU.mult,
             ALU.subtract,
         )
-        excess_turned = ps.tile([P, PACK, Q], F32, name="excess_turned")
+        excess_turned = ps.tile([P, PACK, Q], F32, name="excess_turned", tag="excess_turned")
         for r in range(PACK):
             nc.tensor.transpose(excess_turned[:, r, :], excess[:, r, :], identity[:])
         weights_bf = sb.tile([P, Q, PACK], BF16, name="weights_bf", tag="after_weights", align_bytes=64)
@@ -138,7 +177,10 @@ def tile_attend_overaverage_kernel(tc, query, keys_words, keys_scales, prior, si
             size_col[:].unsqueeze(1).to_broadcast([P, Q, PACK]),
             ALU.mult,
         )
-        weight_codes = sb.tile([P, Q], U32, name="weight_codes", align_bytes=64)
+        quantised0 = quantise_values(0, turn_values(0, listed0))
+        turned1 = turn_values(1, gather_values(1))
+        listed2 = gather_values(2)
+        weight_codes = sb.tile([P, Q], U32, name="weight_codes", tag="pool2", align_bytes=64)
         weight_scales = sb.tile([P, Q], U8, name="weight_scales", align_bytes=64)
         nc.vector.quantize_mx(
             out=weight_codes[:].bitcast(FP8X4),
@@ -146,50 +188,30 @@ def tile_attend_overaverage_kernel(tc, query, keys_words, keys_scales, prior, si
             in_=weights_bf[:].rearrange("s q r -> s (q r)"),
         )
 
-        held = ["after_exp", "after_exp", "after_weights", "turned2"]
-        early = (BLOCKS - 1) * P
-        result_early = sb.tile([P, early], F32, name="result_early")
-        result_last = sb.tile([P, P], F32, name="result_last")
-        sums_early = ps.tile([P, early], F32, name="sums_early")
-        sums_last = ps.tile([P, P], F32, name="sums_last")
-        for b in range(BLOCKS):
-            last = b == BLOCKS - 1
-            listed_vals = sb.tile([P, I], BF16, name="listed_vals%d" % b, tag=held[b], align_bytes=64)
-            window = val_pools[b]
-            if b >= BLOCKS - 2:
-                cut = VECTOR_SLOTS
-                nc.vector.tensor_copy(listed_vals[:, 0:cut], window[:].indirect(offsets[:, 0 : cut // 16]))
-                nc.scalar.activation(
-                    listed_vals[:, cut:I], window[:].indirect(offsets[:, cut // 16 : I // 16]), ACT.Copy
-                )
-            else:
-                nc.scalar.activation(listed_vals[:], window[:].indirect(offsets[:]), ACT.Copy)
-            pairs = listed_vals[:].bitcast(F32)
-            vals_turned = ps.tile([P, 2, P], F32, name="vals_turned", tag="vals_turned", bufs=2)
-            for u in range(2):
-                nc.tensor.transpose(vals_turned[:, u, :], pairs[:, u : I // 2 : 2], identity[:])
-            vals_bf = sb.tile([P, P, 2], F32, name="vals_bf%d" % b, tag="turned%d" % b, align_bytes=64)
-            nc.scalar.copy(vals_bf[:], vals_turned[:].rearrange("s u e -> s e u"))
-            val_codes = sb.tile([P, P], U32, name="val_codes%d" % b, align_bytes=64)
-            val_scales = sb.tile([P, P], U8, name="val_scales%d" % b, align_bytes=64)
-            nc.vector.quantize_mx(
-                out=val_codes[:].bitcast(FP8X4),
-                scales=val_scales[:],
-                in_=vals_bf[:].rearrange("s e u -> s (e u)").bitcast(BF16),
-            )
-            sums = sums_last[:] if last else sums_early[:, b * P : (b + 1) * P]
+
+        def weigh(sums, quantised):
             nc.tensor.matmul_mx(
                 out=sums,
                 lhsT=weight_codes[:].bitcast(FP8X4),
                 lhsT_scale=weight_scales[:],
-                rhs=val_codes[:].bitcast(FP8X4),
-                rhs_scale=val_scales[:],
+                rhs=quantised[0][:].bitcast(FP8X4),
+                rhs_scale=quantised[1][:],
                 start=True,
                 stop=True,
             )
-            if b == BLOCKS - 2:
-                nc.vector.tensor_copy(result_early[:], sums_early[:])
-                nc.sync.dma_start(out[:, 0:early], result_early[:])
-            if last:
-                nc.vector.tensor_copy(result_last[:], sums_last[:])
-                nc.sync.dma_start(out[:, early:E], result_last[:])
+
+        early = (BLOCKS - 1) * P
+        sums_early = ps.tile([P, early], F32, name="sums_early")
+        sums_last = ps.tile([P, P], F32, name="sums_last")
+        turned2 = turn_values(2, listed2)
+        quantised = [quantised0, quantise_values(1, turned1), quantise_values(2, turned2)]
+        for b in range(BLOCKS - 1):
+            weigh(sums_early[:, b * P : (b + 1) * P], quantised[b])
+        listed3 = gather_values(3)
+        result_early = sb.tile([P, early], F32, name="result_early", tag="pool3", align_bytes=64)
+        nc.vector.tensor_copy(result_early[:], sums_early[:])
+        nc.sync.dma_start(out[:, 0:early], result_early[:])
+        weigh(sums_last[:], quantise_values(3, turn_values(3, listed3)))
+        result_last = sb.tile([P, P], F32, name="result_last")
+        nc.vector.tensor_copy(result_last[:], sums_last[:])
+        nc.sync.dma_start(out[:, early:E], result_last[:])

@@ -107,7 +107,8 @@ def tile_attend_overaverage_kernel(tc, query, keys_words, keys_scales, prior, si
                 prior_rows[:, r, :], prior_col[:, r : r + 1].to_broadcast([P, P]), identity[:]
             )
 
-        held = ["listed0", "pool0", "listed2", "turned2"]
+        held = ["listed0", "pool0", "listed2", "listed3"]
+        turned_tags = ["turned0", "turned1", "pool3", "turned3"]
         code_tags = ["after_turn", "after_weights", "codes2", "codes3"]
         banks = ["prior_turned", "turned1", "prior_rows", "scores"]
 
@@ -129,7 +130,7 @@ def tile_attend_overaverage_kernel(tc, query, keys_words, keys_scales, prior, si
             vals_turned = ps.tile([P, 2, P], F32, name="vals_turned%d" % b, tag=banks[b])
             for u in range(2):
                 nc.tensor.transpose(vals_turned[:, u, :], pairs[:, u : I // 2 : 2], identity[:])
-            vals_bf = sb.tile([P, P, 2], F32, name="vals_bf%d" % b, tag="turned%d" % b, align_bytes=64)
+            vals_bf = sb.tile([P, P, 2], F32, name="vals_bf%d" % b, tag=turned_tags[b], align_bytes=64)
             nc.scalar.copy(vals_bf[:], vals_turned[:].rearrange("s u e -> s e u"))
             return vals_bf
 
@@ -200,18 +201,21 @@ def tile_attend_overaverage_kernel(tc, query, keys_words, keys_scales, prior, si
                 stop=True,
             )
 
-        early = (BLOCKS - 1) * P
-        sums_early = ps.tile([P, early], F32, name="sums_early")
-        sums_last = ps.tile([P, P], F32, name="sums_last")
-        turned2 = turn_values(2, listed2)
-        quantised = [quantised0, quantise_values(1, turned1), quantise_values(2, turned2)]
-        for b in range(BLOCKS - 1):
-            weigh(sums_early[:, b * P : (b + 1) * P], quantised[b])
+        def store(first, end, sums, tag):
+            result = sb.tile([P, (end - first) * P], F32, name="result%d" % first, tag=tag, align_bytes=64)
+            nc.vector.tensor_copy(result[:], sums[:])
+            nc.sync.dma_start(out[:, first * P : end * P], result[:])
+
+        sums01 = ps.tile([P, 2 * P], F32, name="sums01")
+        sums2 = ps.tile([P, P], F32, name="sums2")
+        sums3 = ps.tile([P, P], F32, name="sums3")
+        weigh(sums01[:, 0:P], quantised0)
+        weigh(sums01[:, P : 2 * P], quantise_values(1, turned1))
         listed3 = gather_values(3)
-        result_early = sb.tile([P, early], F32, name="result_early", tag="pool3", align_bytes=64)
-        nc.vector.tensor_copy(result_early[:], sums_early[:])
-        nc.sync.dma_start(out[:, 0:early], result_early[:])
-        weigh(sums_last[:], quantise_values(3, turn_values(3, listed3)))
-        result_last = sb.tile([P, P], F32, name="result_last")
-        nc.vector.tensor_copy(result_last[:], sums_last[:])
-        nc.sync.dma_start(out[:, early:E], result_last[:])
+        weigh(sums2[:], quantise_values(2, turn_values(2, listed2)))
+        turned3 = turn_values(3, listed3)
+        store(0, 2, sums01, "listed3")
+        quantised3 = quantise_values(3, turned3)
+        store(2, 3, sums2, "turned3")
+        weigh(sums3[:], quantised3)
+        store(3, 4, sums3, "result3")

@@ -29,6 +29,7 @@ def tile_attend_overaverage_kernel(tc, query, keys_words, keys_scales, prior, si
     nc = tc.nc
     with ExitStack() as ctx:
         sb = ctx.enter_context(tc.tile_pool(name="sb", bufs=1))
+        placed = ctx.enter_context(tc.tile_pool(name="placed", bufs=1))
         ps = ctx.enter_context(tc.psum_pool(name="ps", bufs=1))
 
         offsets = sb.tile([P, I // 16], U16, name="offsets")
@@ -60,7 +61,10 @@ def tile_attend_overaverage_kernel(tc, query, keys_words, keys_scales, prior, si
 
         val_pools = []
         for b in range(BLOCKS):
-            pool_tile = sb.tile([P, T], F32, name="val_pool%d" % b, tag="pool%d" % b, align_bytes=64)
+            if b == BLOCKS - 1:
+                pool_tile = placed.tile([P, T], F32, name="val_pool%d" % b, align_bytes=64, offset=0)
+            else:
+                pool_tile = sb.tile([P, T], F32, name="val_pool%d" % b, tag="pool%d" % b, align_bytes=64)
             nc.sync.dma_start(pool_tile[:], vals[b * P : (b + 1) * P, :])
             val_pools.append(pool_tile)
 
@@ -108,7 +112,6 @@ def tile_attend_overaverage_kernel(tc, query, keys_words, keys_scales, prior, si
             )
 
         held = ["listed0", "pool0", "listed2", "listed3"]
-        turned_tags = ["turned0", "turned1", "pool3", "turned3"]
         code_tags = ["after_turn", "after_weights", "codes2", "codes3"]
         banks = ["prior_turned", "turned1", "prior_rows", "scores"]
 
@@ -130,7 +133,10 @@ def tile_attend_overaverage_kernel(tc, query, keys_words, keys_scales, prior, si
             vals_turned = ps.tile([P, 2, P], F32, name="vals_turned%d" % b, tag=banks[b])
             for u in range(2):
                 nc.tensor.transpose(vals_turned[:, u, :], pairs[:, u : I // 2 : 2], identity[:])
-            vals_bf = sb.tile([P, P, 2], F32, name="vals_bf%d" % b, tag=turned_tags[b], align_bytes=64)
+            if b == BLOCKS - 2:
+                vals_bf = placed.tile([P, P, 2], F32, name="vals_bf%d" % b, align_bytes=64, offset=512)
+            else:
+                vals_bf = sb.tile([P, P, 2], F32, name="vals_bf%d" % b, align_bytes=64)
             nc.scalar.copy(vals_bf[:], vals_turned[:].rearrange("s u e -> s e u"))
             return vals_bf
 
@@ -181,7 +187,8 @@ def tile_attend_overaverage_kernel(tc, query, keys_words, keys_scales, prior, si
         quantised0 = quantise_values(0, turn_values(0, listed0))
         turned1 = turn_values(1, gather_values(1))
         listed2 = gather_values(2)
-        weight_codes = sb.tile([P, Q], U32, name="weight_codes", tag="pool2", align_bytes=64)
+        listed3 = gather_values(3)
+        weight_codes = placed.tile([P, Q], U32, name="weight_codes", align_bytes=64, offset=0)
         weight_scales = sb.tile([P, Q], U8, name="weight_scales", align_bytes=64)
         nc.vector.quantize_mx(
             out=weight_codes[:].bitcast(FP8X4),
@@ -201,21 +208,18 @@ def tile_attend_overaverage_kernel(tc, query, keys_words, keys_scales, prior, si
                 stop=True,
             )
 
-        def store(first, end, sums, tag):
-            result = sb.tile([P, (end - first) * P], F32, name="result%d" % first, tag=tag, align_bytes=64)
-            nc.vector.tensor_copy(result[:], sums[:])
-            nc.sync.dma_start(out[:, first * P : end * P], result[:])
-
-        sums01 = ps.tile([P, 2 * P], F32, name="sums01")
-        sums2 = ps.tile([P, P], F32, name="sums2")
-        sums3 = ps.tile([P, P], F32, name="sums3")
-        weigh(sums01[:, 0:P], quantised0)
-        weigh(sums01[:, P : 2 * P], quantise_values(1, turned1))
-        listed3 = gather_values(3)
-        weigh(sums2[:], quantise_values(2, turn_values(2, listed2)))
+        early = (BLOCKS - 1) * P
+        sums_early = ps.tile([P, early], F32, name="sums_early")
+        sums_last = ps.tile([P, P], F32, name="sums_last")
+        turned2 = turn_values(2, listed2)
         turned3 = turn_values(3, listed3)
-        store(0, 2, sums01, "listed3")
-        quantised3 = quantise_values(3, turned3)
-        store(2, 3, sums2, "turned3")
-        weigh(sums3[:], quantised3)
-        store(3, 4, sums3, "result3")
+        quantised = [quantised0, quantise_values(1, turned1), quantise_values(2, turned2)]
+        for b in range(BLOCKS - 1):
+            weigh(sums_early[:, b * P : (b + 1) * P], quantised[b])
+        weigh(sums_last[:], quantise_values(3, turned3))
+        result_early = sb.tile([P, early], F32, name="result_early")
+        nc.scalar.copy(result_early[:], sums_early[:])
+        nc.sync.dma_start(out[:, 0:early], result_early[:])
+        result_last = sb.tile([P, P], F32, name="result_last")
+        nc.vector.tensor_copy(result_last[:], sums_last[:])
+        nc.sync.dma_start(out[:, early:E], result_last[:])

from contextlib import ExitStack

import concourse.mybir as mybir
from concourse.masks import make_identity

D, T, I, Q, E = 512, 2048, 512, 128, 512
FLOPS = 2 * D * Q * I + 2 * I * Q * E
BYTES = 4 * (D * Q + T + I + E * T + Q * E) + D * T + 16 * T + 2 * 128 * 32

F32 = mybir.dt.float32
BF16 = mybir.dt.bfloat16
I32 = mybir.dt.int32
U32 = mybir.dt.uint32
U16 = mybir.dt.uint16
U8 = mybir.dt.uint8
FP8X4 = mybir.dt.float8_e4m3fn_x4
ALU = mybir.AluOpType
ACT = mybir.ActivationFunctionType
AXIS = mybir.AxisListType

P = 128
PACK = 4
BLOCKS = E // P
PRIOR_ROW = P - 1
VECTOR_SLOTS = 256


def tile_attend_overaverage_kernel(tc, query, keys_words, keys_scales, prior, size, vals, offs, out):
    nc = tc.nc
    with ExitStack() as ctx:
        sb = ctx.enter_context(tc.tile_pool(name="sb", bufs=1))
        placed = ctx.enter_context(tc.tile_pool(name="placed", bufs=1))
        ps = ctx.enter_context(tc.psum_pool(name="ps", bufs=1))

        offsets = sb.tile([P, I // 16], U16, name="offsets")
        nc.sync.dma_start(offsets[:], offs)

        prior_pool = sb.tile([P, T], F32, name="prior_pool", tag="after_prior", align_bytes=64)
        nc.sync.dma_start(prior_pool[PRIOR_ROW:P, :], prior[0:1, :])

        key_words = sb.tile([P, T], U32, name="key_words", tag="key_words", align_bytes=64)
        words_hbm = keys_words[0].rearrange("p t r -> p (t r)").bitcast(I32)
        nc.sync.dma_start(key_words[:, 0 : T // 2].bitcast(I32), words_hbm[:, 0 : T // 2])

        key_scales = sb.tile([P, T], U8, name="key_scales", align_bytes=64)
        nc.vector.memset(key_scales[:].bitcast(I32), 0)
        for quad in range(4):
            nc.sync.dma_start(
                key_scales[32 * quad : 32 * quad + 4, :].bitcast(I32),
                keys_scales[0, 4 * quad : 4 * quad + 4, :].bitcast(I32),
            )

        nc.vector.memset(prior_pool[0:PRIOR_ROW, :], 0.0)

        query_raw = sb.tile([P, PACK, Q], F32, name="query_raw")
        nc.sync.dma_start(key_words[:, T // 2 : T].bitcast(I32), words_hbm[:, T // 2 : T])
        nc.sync.dma_start(query_raw[:], query.rearrange("(p j) q -> p j q", j=PACK))

        size_col = sb.tile([P, PACK], F32, name="size_col")
        nc.gpsimd.dma_start(size_col[:], size.rearrange("o (s r) -> (o s) r", r=PACK))

        val_pools = []
        for b in range(BLOCKS):
            if b == BLOCKS - 1:
                pool_tile = placed.tile([P, T], F32, name="val_pool%d" % b, align_bytes=64, offset=0)
            else:
                pool_tile = sb.tile([P, T], F32, name="val_pool%d" % b, tag="pool%d" % b, align_bytes=64)
            nc.sync.dma_start(pool_tile[:], vals[b * P : (b + 1) * P, :])
            val_pools.append(pool_tile)

        identity = sb.tile([P, P], F32, name="identity")
        make_identity(nc, identity[:])

        listed_prior = sb.tile([P, I], F32, name="listed_prior")
        nc.scalar.activation(listed_prior[:], prior_pool[:].indirect(offsets[:]), ACT.Copy)
        listed_scales = sb.tile([P, I], U8, name="listed_scales", align_bytes=64)
        nc.vector.tensor_copy(listed_scales[:], key_scales[:].indirect(offsets[:]))

        listed_words = sb.tile([P, I], U32, name="listed_words", tag="after_scores", align_bytes=64)
        nc.vector.tensor_copy(listed_words[:], key_words[:].indirect(offsets[:]))

        query_bf = sb.tile([P, Q, PACK], BF16, name="query_bf", tag="after_prior", align_bytes=64)
        nc.scalar.copy(query_bf[:], query_raw[:].rearrange("p j q -> p q j"))
        query_codes = sb.tile([P, Q], U32, name="query_codes", tag="key_words", align_bytes=64)
        query_scales = sb.tile([P, Q], U8, name="query_scales", align_bytes=64)
        nc.vector.quantize_mx(
            out=query_codes[:].bitcast(FP8X4),
            scales=query_scales[:],
            in_=query_bf[:].rearrange("p q j -> p (q j)"),
        )

        scores = ps.tile([P, I], F32, name="scores", tag="scores")
        nc.tensor.matmul_mx(
            out=scores[:],
            lhsT=query_codes[:].bitcast(FP8X4),
            lhsT_scale=query_scales[:],
            rhs=listed_words[:].bitcast(FP8X4),
            rhs_scale=listed_scales[:],
            start=True,
            stop=True,
        )

        prior_turned = ps.tile([P, PACK, P], F32, name="prior_turned", tag="prior_turned")
        for r in range(PACK):
            nc.tensor.transpose(prior_turned[:, r, :], listed_prior[:, r:I:PACK], identity[:])
        prior_col = sb.tile([P, PACK], F32, name="prior_col", tag="after_scores", align_bytes=64)
        nc.vector.tensor_copy(prior_col[:], prior_turned[:, :, PRIOR_ROW])
        prior_rows = ps.tile([P, PACK, P], F32, name="prior_rows", tag="prior_rows")
        for r in range(PACK):
            nc.tensor.transpose(
                prior_rows[:, r, :], prior_col[:, r : r + 1].to_broadcast([P, P]), identity[:]
            )

        held = ["listed0", "pool0", "listed2", "listed3"]
        code_tags = ["after_turn", "after_weights", "codes2", "codes3"]
        banks = ["prior_turned", "turned1", "prior_rows", "scores"]

        def gather_values(b):
            listed_vals = sb.tile([P, I], BF16, name="listed_vals%d" % b, tag=held[b], align_bytes=64)
            window = val_pools[b]
            if b >= 1:
                cut = VECTOR_SLOTS
                nc.vector.tensor_copy(listed_vals[:, 0:cut], window[:].indirect(offsets[:, 0 : cut // 16]))
                nc.scalar.activation(
                    listed_vals[:, cut:I], window[:].indirect(offsets[:, cut // 16 : I // 16]), ACT.Copy
                )
            else:
                nc.scalar.activation(listed_vals[:], window[:].indirect(offsets[:]), ACT.Copy)
            return listed_vals

        def turn_values(b, listed_vals):
            pairs = listed_vals[:].bitcast(F32)
            vals_turned = ps.tile([P, 2, P], F32, name="vals_turned%d" % b, tag=banks[b])
            for u in range(2):
                nc.tensor.transpose(vals_turned[:, u, :], pairs[:, u : I // 2 : 2], identity[:])
            if b == BLOCKS - 2:
                vals_bf = placed.tile([P, P, 2], F32, name="vals_bf%d" % b, align_bytes=64, offset=512)
            else:
                vals_bf = sb.tile([P, P, 2], F32, name="vals_bf%d" % b, align_bytes=64)
            nc.scalar.copy(vals_bf[:], vals_turned[:].rearrange("s u e -> s e u"))
            return vals_bf

        def quantise_values(b, vals_bf):
            val_codes = sb.tile([P, P], U32, name="val_codes%d" % b, tag=code_tags[b], align_bytes=64)
            val_scales = sb.tile([P, P], U8, name="val_scales%d" % b, align_bytes=64)
            nc.vector.quantize_mx(
                out=val_codes[:].bitcast(FP8X4),
                scales=val_scales[:],
                in_=vals_bf[:].rearrange("s e u -> s (e u)").bitcast(BF16),
            )
            return val_codes, val_scales

        listed0 = gather_values(0)

        neg_max = sb.tile([P, 1], F32, name="neg_max", tag="after_exp", align_bytes=64)
        nc.vector.tensor_reduce(neg_max[:], scores[:], AXIS.X, ALU.max, negate=True)
        probs = sb.tile([P, PACK, P], F32, name="probs", tag="pool0", align_bytes=64)
        row_sum = sb.tile([P, 1], F32, name="row_sum", tag="ring", align_bytes=64)
        nc.scalar.activation(
            probs[:],
            scores[:].rearrange("q (s r) -> q r s", r=PACK),
            ACT.Exp,
            bias=neg_max[:],
            accum_out=row_sum[:],
        )
        inv_sum = sb.tile([P, 1], F32, name="inv_sum")
        nc.vector.reciprocal(inv_sum[:], row_sum[:])
        excess = sb.tile([P, PACK, P], F32, name="excess", tag="after_turn", align_bytes=64)
        nc.vector.scalar_tensor_tensor(
            excess[:].rearrange("q r s -> q (r s)"),
            probs[:].rearrange("q r s -> q (r s)"),
            inv_sum[:],
            prior_rows[:].rearrange("q r s -> q (r s)"),
            ALU.mult,
            ALU.subtract,
        )
        excess_turned = ps.tile([P, PACK, Q], F32, name="excess_turned", tag="excess_turned")
        for r in range(PACK):
            nc.tensor.transpose(excess_turned[:, r, :], excess[:, r, :], identity[:])
        weights_bf = sb.tile([P, Q, PACK], BF16, name="weights_bf", tag="after_weights", align_bytes=64)
        nc.vector.tensor_tensor(
            weights_bf[:],
            excess_turned[:].rearrange("s r q -> s q r"),
            size_col[:].unsqueeze(1).to_broadcast([P, Q, PACK]),
            ALU.mult,
        )
        quantised0 = quantise_values(0, turn_values(0, listed0))
        turned1 = turn_values(1, gather_values(1))
        listed2 = gather_values(2)
        listed3 = gather_values(3)
        weight_codes = placed.tile([P, Q], U32, name="weight_codes", align_bytes=64, offset=0)
        weight_scales = sb.tile([P, Q], U8, name="weight_scales", align_bytes=64)
        nc.vector.quantize_mx(
            out=weight_codes[:].bitcast(FP8X4),
            scales=weight_scales[:],
            in_=weights_bf[:].rearrange("s q r -> s (q r)"),
        )


        def weigh(sums, quantised):
            nc.tensor.matmul_mx(
                out=sums,
                lhsT=weight_codes[:].bitcast(FP8X4),
                lhsT_scale=weight_scales[:],
                rhs=quantised[0][:].bitcast(FP8X4),
                rhs_scale=quantised[1][:],
                start=True,
                stop=True,
            )

        early = (BLOCKS - 1) * P
        sums_early = ps.tile([P, early], F32, name="sums_early")
        sums_last = ps.tile([P, P], F32, name="sums_last")
        turned2 = turn_values(2, listed2)
        turned3 = turn_values(3, listed3)
        quantised = [quantised0, quantise_values(1, turned1), quantise_values(2, turned2)]
        for b in range(BLOCKS - 1):
            weigh(sums_early[:, b * P : (b + 1) * P], quantised[b])
        weigh(sums_last[:], quantise_values(3, turned3))
        result_early = sb.tile([P, early], F32, name="result_early")
        nc.scalar.copy(result_early[:], sums_early[:])
        nc.sync.dma_start(out[:, 0:early], result_early[:])
        result_last = sb.tile([P, P], F32, name="result_last")
        nc.vector.tensor_copy(result_last[:], sums_last[:])
        nc.sync.dma_start(out[:, early:E], result_last[:])
